import numpy as np
import ml_dtypes


def mxq(x, axis, fmt="e4m3"):
    dtype, down = {"e4m3": (ml_dtypes.float8_e4m3fn, 7), "e5m2": (ml_dtypes.float8_e5m2, 14)}[fmt]
    v = np.moveaxis(np.asarray(x, np.float32).astype(ml_dtypes.bfloat16).astype(np.float64), axis, -1)
    blocks = v.reshape(v.shape[:-1] + (-1, 32))
    amax = np.abs(blocks).max(-1, keepdims=True)
    byte = np.maximum(np.where(amax > 0, np.frexp(amax)[1] - 1 + 127, 0) - down, 1)
    scale = np.exp2(byte - 127.0)
    codes = (blocks / scale).astype(np.float32).astype(dtype).astype(np.float64)
    return np.moveaxis((codes * scale).reshape(v.shape), -1, axis)


WIDE = False


def mx_kscale(k):
    if not WIDE:
        return np.ones(k)
    levels = np.array([10, -10, 5, -5, 0])
    if k % 512:
        return np.exp2(np.random.permutation(np.resize(levels, k // 32))).repeat(32)
    a = np.empty((k // 512, 16))
    for p in range(k // 512):
        a[p, :8] = np.random.permutation(np.resize(levels, 8))
        for g in range(8):
            far = levels[np.abs(levels - a[p, g]) >= 10]
            a[p, g + 8] = far[np.random.randint(len(far))]
    return np.exp2(a.ravel()).repeat(32)


def f64(x):
    return np.asarray(x).astype(np.float64)


def striped(idx):
    return np.tile(idx.reshape(-1, 16).T, (8, 1)).astype(np.uint16)


def unstriped(offs):
    return offs[:16].T.reshape(-1).astype(np.int64)


E2M1 = np.array([0.0, 0.5, 1.0, 1.5, 2.0, 3.0, 4.0, 6.0, -0.0, -0.5, -1.0, -1.5, -2.0, -3.0, -4.0, -6.0])


def pack_weight(w, fmt):
    k, n = w.shape
    w = f64(np.asarray(w, np.float32).astype(ml_dtypes.bfloat16)).reshape(k // 32, 32, n)
    amax = np.abs(w).max(1)
    if fmt == "e4m3":
        byte = np.frexp(amax)[1] - 1 + 127 - 7
    else:
        mant, ex = np.frexp(amax / 6.0)
        byte = np.where(mant > 0.5, ex, ex - 1) + 127
    byte = np.clip(np.where(amax > 0, byte, 1), 1, 254)
    scaled = (w * np.exp2(127.0 - byte)[:, None, :]).reshape(k, n).astype(np.float32)
    by_word = np.ascontiguousarray(scaled.reshape(k // 512, 128, 4, n).transpose(0, 1, 3, 2))
    if fmt == "e4m3":
        words = by_word.astype(ml_dtypes.float8_e4m3fn).view(np.uint8)
    else:
        c = by_word.astype(ml_dtypes.float4_e2m1fn).view(np.uint8) & 0xF
        words = (c[..., 0::2] | (c[..., 1::2] << 4)).reshape(k // 512, 128, 2 * n)
    return np.ascontiguousarray(words), np.ascontiguousarray(byte.astype(np.uint8).reshape(k // 512, 16, n))


def unpack_weight(words, scales, fmt):
    g, _, n = scales.shape
    words = np.ascontiguousarray(words).reshape(g, 128, n, -1)
    if fmt == "e4m3":
        vals = words.view(ml_dtypes.float8_e4m3fn).astype(np.float64)
    else:
        nib = np.empty((g, 128, n, 4), np.uint8)
        nib[..., 0::2] = words & 0xF
        nib[..., 1::2] = words >> 4
        vals = E2M1[nib]
    vals = vals * np.repeat(np.exp2(scales.astype(np.float64) - 127.0), 8, axis=1)[..., None]
    return vals.transpose(0, 1, 3, 2).reshape(g * 512, n)


def gelu(v):
    return 0.5 * v * (1.0 + np.tanh(np.sqrt(2.0 / np.pi) * (v + 0.044715 * v**3)))


def striped8(idx):
    return np.concatenate([v.reshape(-1, 16).T for v in idx]).astype(np.uint16)


def unstriped8(offs):
    return np.stack([offs[16 * g:16 * g + 16].T.reshape(-1) for g in range(8)]).astype(np.int64)


def heads(h, wgt, idx8):
    r = np.arange(h.shape[0])
    return wgt[r // 4 % 128] * h[r[:, None], idx8[r % 512 // 64]]


def put_heads(h, wgs, idx8, t2):
    r = np.arange(h.shape[0])
    page = np.zeros((h.shape[0], t2))
    page[r[:, None], idx8[r % 512 // 64]] = wgs[r // 4 % 128] * h
    return page


K, T, S, H, P, T2, N = 512, 4096, 1024, 1024, 512, 1024, 512

def setup_inputs():
    n = np.random.standard_normal
    s = mx_kscale(K)[:, None]
    u = mx_kscale(H)[:, None]
    d = {}
    d["tab_words"], d["tab_scales"] = pack_weight(n((K, T)) * s, "e4m3")
    d["offs"] = striped(np.random.permutation(T)[:S])
    d["w1"] = (n((K, H)) / s * u.T / K ** 0.5).astype(np.float32)
    d["w2_words"], d["w2_scales"] = pack_weight(n((K, H)) / s / K ** 0.5, "e2m1")
    d["w3"] = (n((K, H)) / s * u.T / K ** 0.5).astype(np.float32)
    d["wgt"] = np.repeat(np.random.uniform(0.5, 2.0, (8, P)), 16, axis=0).astype(np.float32)
    d["offs2"] = striped8(np.stack([np.random.permutation(S)[:P] for _ in range(8)]))
    d["shift"] = (n(H) * u[:, 0]).astype(np.float32)
    d["w4_words"], d["w4_scales"] = pack_weight(n((H, N)) / u / H ** 0.5, "e2m1")
    d["w5"] = (n((H, N)) / u / H ** 0.5).astype(np.float32)
    d["gain"] = np.exp(0.4 * n(N)).astype(np.float32)
    d["wgo"] = np.repeat(np.random.uniform(0.5, 2.0, (8, P)), 16, axis=0).astype(np.float32)
    d["offs3"] = striped8(np.stack([np.random.permutation(T2)[:P] for _ in range(8)]))
    return d

def reference(tab_words, tab_scales, offs, w1, w2_words, w2_scales, w3, wgt, offs2, shift, w4_words, w4_scales, w5, gain, wgo, offs3):
    v = unpack_weight(tab_words, tab_scales, "e4m3")[:, unstriped(offs)]
    w2 = unpack_weight(w2_words, w2_scales, "e2m1")
    w4 = unpack_weight(w4_words, w4_scales, "e2m1")
    a = mxq(f64(w1), 0, "e4m3").T @ v
    b = w2.T @ v
    base = mxq(f64(w3), 0, "e4m3").T @ v
    h = np.maximum(a * b, base) + a
    x = heads(h, f64(wgt), unstriped8(offs2)) + f64(shift)[:, None]
    xq = mxq(x, 0, "e4m3")
    y1 = w4.T @ xq
    y2 = mxq(f64(w5), 0, "e4m3").T @ xq
    y = np.minimum(y1, y2) * f64(gain)[:, None]
    return put_heads(y, f64(wgo), unstriped8(offs3), T2)

from contextlib import ExitStack

import concourse.mybir as mybir

K, T, S, H, M, T2, N = 512, 4096, 1024, 1024, 512, 1024, 512
FLOPS = 2 * (3 * K * H * S + 2 * H * N * M)

F32 = mybir.dt.float32
BF16 = mybir.dt.bfloat16
I32 = mybir.dt.int32
U32 = mybir.dt.uint32
U16 = mybir.dt.uint16
U8 = mybir.dt.uint8
FP8X4 = mybir.dt.float8_e4m3fn_x4
FP4X4 = mybir.dt.float4_e2m1fn_x4
ALU = mybir.AluOpType
ACT = mybir.ActivationFunctionType

P = 128
PACK = 4
BLK = P * PACK
BANK = 512
SUMMED_IN_PSUM = 6


def tile_list_shelter_need_slots_kernel(
    tc, tab_words, tab_scales, offs, w1, w2_words, w2_scales, w3, wgt, offs2, shift,
    w4_words, w4_scales, w5, gain, wgo, offs3, out,
):
    nc = tc.nc
    with ExitStack() as ctx:
        keep = ctx.enter_context(tc.tile_pool(name="keep", bufs=1))
        ring = ctx.enter_context(tc.tile_pool(name="ring", bufs=2))
        psum = ctx.enter_context(tc.psum_pool(name="psum", bufs=1))

        def load_scale_rows(queue, plane, rows):
            passes = rows.shape[0]
            for q in range(4):
                queue.dma_start(
                    out=plane[32 * q : 32 * q + 4, :].bitcast(I32).rearrange("r (a c) -> r a c", a=passes),
                    in_=rows[:, 4 * q : 4 * q + 4, :].bitcast(I32).rearrange("a r c -> r a c"),
                )

        def deal_columns(dst, src):
            nc.vector.tensor_copy(
                out=dst.rearrange("p (b t m) -> p b m t", t=PACK, m=P),
                in_=src.rearrange("p (b m t) -> p b m t", t=PACK, m=P),
            )

        def load_weight(rows, name):
            raw = keep.tile([P, PACK, BLK], F32, name=name + "_raw")
            nc.sync.dma_start(out=raw[:], in_=rows.rearrange("(p j) c -> p j c", j=PACK))
            return raw

        def group_weight(raw, name, shared=False):
            grouped = keep.tile([P, PACK * BLK], BF16, name=name + "_grouped", align_bytes=64)
            dst = grouped[:].rearrange("p (t m j) -> p m j t", t=PACK, j=PACK)
            src = raw[:].rearrange("p j (m t) -> p m j t", t=PACK)
            nc.scalar.activation(dst[:, 0 : P // 2], src[:, 0 : P // 2], ACT.Identity)
            if shared:
                nc.vector.tensor_copy(dst[:, P // 2 : P], src[:, P // 2 : P])
            else:
                nc.scalar.activation(dst[:, P // 2 : P], src[:, P // 2 : P], ACT.Identity)
            return grouped

        def quantize(grouped, codes, name):
            plane = keep.tile([P, BLK], U8, name=name + "_plane", align_bytes=64)
            nc.vector.quantize_mx(out=codes.bitcast(FP8X4), scales=plane[:], in_=grouped[:])
            return codes, plane

        def quantize_weight(raw, name, shared=False):
            codes = keep.tile([P, BLK], U32, name=name + "_codes", align_bytes=64)
            return quantize(group_weight(raw, name, shared), codes[:], name)

        tab_plane = keep.tile([P, T], U8, align_bytes=64)
        nc.vector.memset(tab_plane[:].bitcast(I32), 0)
        w2_plane_raw = keep.tile([P, H], U8, align_bytes=64)
        nc.vector.memset(w2_plane_raw[:].bitcast(I32), 0)
        w4_plane_raw = keep.tile([P, 2 * N], U8, align_bytes=64)
        nc.vector.memset(w4_plane_raw[:].bitcast(I32), 0)

        list1 = keep.tile([P, S // 16], U16)
        nc.sync.dma_start(list1[:], offs)
        w1_raw = [load_weight(w1[:, 0:BLK], "w1_0")]
        w2_raw = keep.tile([P, 2 * H], U8, align_bytes=64)
        nc.sync.dma_start(out=w2_raw[:].bitcast(I32), in_=w2_words[0].bitcast(I32))
        load_scale_rows(nc.sync, tab_plane, tab_scales)
        tab = keep.tile([P, T], I32, align_bytes=64)
        nc.sync.dma_start(out=tab[:], in_=tab_words[0].rearrange("p c i -> p (c i)").bitcast(I32))
        load_scale_rows(nc.sync, w2_plane_raw, w2_scales)
        w3_raw = [load_weight(w3[:, 0:BLK], "w3_0")]
        wgt_sb = keep.tile([P, M], F32, tag="wgt_then_w4", align_bytes=64)
        nc.sync.dma_start(out=wgt_sb[:], in_=wgt)
        list2 = keep.tile([P, M // 16], U16)
        nc.sync.dma_start(list2[:], offs2)
        shift_sb = keep.tile([P, 2, PACK], F32)
        nc.sync.dma_start(out=shift_sb[:], in_=shift.rearrange("(b p t) -> p b t", p=P, t=PACK))
        w1_raw.append(load_weight(w1[:, BLK : 2 * BLK], "w1_1"))
        w3_raw.append(load_weight(w3[:, BLK : 2 * BLK], "w3_1"))
        w4_raw = keep.tile([P, 2 * 2 * N], U8, align_bytes=64)
        nc.sync.dma_start(
            out=w4_raw[:].bitcast(I32).rearrange("p (a c) -> p a c", a=2),
            in_=w4_words.bitcast(I32).rearrange("a p c -> p a c"),
        )
        load_scale_rows(nc.sync, w4_plane_raw, w4_scales)
        w5_raw = [load_weight(w5[a * BLK : (a + 1) * BLK, :], "w5_%d" % a) for a in range(2)]
        wgo_sb = keep.tile([P, M], F32)
        nc.sync.dma_start(out=wgo_sb[:], in_=wgo)
        gain_sb = keep.tile([P, PACK], F32)
        nc.sync.dma_start(out=gain_sb[:], in_=gain.rearrange("(p t) -> p t", t=PACK))
        list3 = keep.tile([P, M // 16], U16)
        nc.sync.dma_start(list3[:], offs3)

        w2_codes = keep.tile([P, 2 * H], U8, align_bytes=64)
        deal_columns(w2_codes[:].bitcast(U16), w2_raw[:].bitcast(U16))
        w1_q = [quantize_weight(w1_raw[0], "w1_0")]
        v_plane = keep.tile([P, S], U8, align_bytes=64)
        nc.vector.tensor_copy(v_plane[:], tab_plane[:].indirect(list1[:]))
        w2_plane = keep.tile([P, H], U8, align_bytes=64)
        deal_columns(w2_plane[:], w2_plane_raw[:])
        v_codes = []
        for half in range(2):
            picked = keep.tile([P, BANK], U32, name="v_codes%d" % half, align_bytes=64)
            cols = slice(half * BANK // 16, (half + 1) * BANK // 16)
            nc.vector.tensor_copy(picked[:], tab[:].bitcast(U32).indirect(list1[:, cols]))
            v_codes.append(picked)
        w3_q = [quantize_weight(w3_raw[0], "w3_0", shared=True)]

        def first_stage(b, t):
            cols = slice(t * P, (t + 1) * P)
            wide = slice(b * BLK + t * P, b * BLK + (t + 1) * P)
            wide2 = slice(2 * wide.start, 2 * wide.stop)
            if PACK * b + t == 2 * PACK - 1:
                h = keep.tile([P, S], F32, name="last_h", tag="h_then_w5", align_bytes=64)
            else:
                h = ring.tile([P, S], F32, name="h", bufs=3)
            parts = []
            for half in (1, 0):
                js = slice(half * BANK, (half + 1) * BANK)
                moving = dict(rhs=v_codes[half][:].bitcast(FP8X4), rhs_scale=v_plane[:, js])
                w1_op = dict(lhsT=w1_q[b][0][:, cols].bitcast(FP8X4), lhsT_scale=w1_q[b][1][:, cols])
                w3_op = dict(lhsT=w3_q[b][0][:, cols].bitcast(FP8X4), lhsT_scale=w3_q[b][1][:, cols])
                in_psum = half == 1 and PACK * b + t >= 2 * PACK - SUMMED_IN_PSUM
                a_ps = psum.tile([P, BANK], F32, name="a_ps", bufs=2)
                nc.tensor.matmul_mx(out=a_ps[:], start=True, stop=True, **w1_op, **moving)
                b_ps = psum.tile([P, BANK], F32, name="b_ps", bufs=3)
                nc.tensor.matmul_mx(
                    out=b_ps[:], lhsT=w2_codes[:, wide2].bitcast(FP4X4), lhsT_scale=w2_plane[:, wide],
                    start=True, stop=True, **moving,
                )
                c_ps = psum.tile([P, BANK], F32, name="c_ps", bufs=3)
                if in_psum:
                    nc.tensor.matmul_mx(out=c_ps[:], start=True, stop=False, **w1_op, **moving)
                nc.tensor.matmul_mx(out=c_ps[:], start=not in_psum, stop=True, **w3_op, **moving)
                a_sb = ring.tile([P, BANK], F32, name="a_sb", bufs=8)
                nc.scalar.copy(a_sb[:], a_ps[:])
                parts.append((js, in_psum, a_sb, b_ps, c_ps))
            prods = []
            for js, in_psum, a_sb, b_ps, c_ps in parts:
                prod = ring.tile([P, BANK], F32, name="prod", bufs=8)
                if in_psum:
                    nc.vector.scalar_tensor_tensor(prod[:], b_ps[:], 1.0, a_sb[:], ALU.add, ALU.mult)
                else:
                    nc.vector.tensor_tensor(prod[:], b_ps[:], a_sb[:], ALU.mult)
                prods.append(prod)
            larger = []
            for (js, in_psum, a_sb, b_ps, c_ps), prod in zip(parts, prods):
                if in_psum:
                    nc.vector.tensor_tensor(h[:, js], c_ps[:], prod[:], ALU.max)
                else:
                    top = ring.tile([P, BANK], F32, name="top", bufs=3)
                    nc.vector.tensor_tensor(top[:], c_ps[:], prod[:], ALU.max)
                    larger.append((js, top, a_sb))
            for js, top, a_sb in larger:
                nc.vector.tensor_tensor(h[:, js], top[:], a_sb[:], ALU.add)
            return h

        def pick(h, b, t, x_rows):
            picked = ring.tile([P, M], F32, name="picked", bufs=3)
            nc.vector.tensor_tensor(picked[:], h[:].indirect(list2[:]), wgt_sb[:], ALU.mult)
            nc.scalar.activation(x_rows[:, t, :], picked[:], ACT.Identity, bias=shift_sb[:, b, t : t + 1])

        def group_x(x_rows, b, shared=False):
            grouped = keep.tile([P, PACK * M], BF16, name="x_grouped%d" % b, align_bytes=64)
            dst = grouped[:].rearrange("p (c i t) -> p c t i", t=PACK, i=4)
            src = x_rows[:].rearrange("p t (c i) -> p c t i", i=4)
            nc.scalar.copy(dst[:, 0 : P // 2], src[:, 0 : P // 2])
            if shared:
                nc.vector.tensor_copy(dst[:, P // 2 : P], src[:, P // 2 : P])
            else:
                nc.scalar.copy(dst[:, P // 2 : P], src[:, P // 2 : P])
            return grouped

        def quantize_x(x_rows, b, shared=False):
            codes = keep.tile([P, M], U32, name="x_codes%d" % b, align_bytes=64)
            return quantize(group_x(x_rows, b, shared), codes[:], "x%d" % b)

        x_rows = [keep.tile([P, PACK, M], BF16, name="x_rows%d" % b) for b in range(2)]
        x_q = []
        waiting = None
        for b in range(2):
            for t in range(PACK):
                h = first_stage(b, t)
                if waiting is not None:
                    pick(*waiting)
                waiting = (h, b, t, x_rows[b])
                if b == 0 and t == 1:
                    w1_q.append(quantize_weight(w1_raw[1], "w1_1"))
                if b == 0 and t == 2:
                    w3_q.append(quantize_weight(w3_raw[1], "w3_1"))
                if b == 1 and t == 0:
                    x_q.append(quantize_x(x_rows[0], 0))
        w5_grouped = [group_weight(w5_raw[a], "w5_%d" % a) for a in range(2)]
        w4_plane = keep.tile([P, 2 * N], U8, align_bytes=64)
        deal_columns(w4_plane[:], w4_plane_raw[:])
        pick(*waiting)
        w5_codes = keep.tile([P, 2 * N], U32, tag="h_then_w5", align_bytes=64)
        w5_q = [quantize(w5_grouped[a], w5_codes[:, a * N : (a + 1) * N], "w5_%d" % a) for a in range(2)]
        w4_codes = keep.tile([P, 2 * 2 * N], U8, tag="wgt_then_w4", align_bytes=64)
        deal_columns(w4_codes[:].bitcast(U16), w4_raw[:].bitcast(U16))
        x_q.append(quantize_x(x_rows[1], 1, shared=True))

        out_rows = out.rearrange("(p t) c -> p t c", t=PACK)
        for t in range(PACK):
            cols = slice(t * P, (t + 1) * P)
            y1_ps = psum.tile([P, BANK], F32, name="b_ps", bufs=3)
            y2_ps = psum.tile([P, BANK], F32, name="c_ps", bufs=3)
            for a in range(2):
                wide = slice(a * N + t * P, a * N + (t + 1) * P)
                nc.tensor.matmul_mx(
                    out=y1_ps[:], lhsT=w4_codes[:, 2 * wide.start : 2 * wide.stop].bitcast(FP4X4),
                    lhsT_scale=w4_plane[:, wide], rhs=x_q[a][0].bitcast(FP8X4), rhs_scale=x_q[a][1][:],
                    start=a == 0, stop=a == 1,
                )
            for a in range(2):
                nc.tensor.matmul_mx(
                    out=y2_ps[:], lhsT=w5_q[a][0][:, cols].bitcast(FP8X4), lhsT_scale=w5_q[a][1][:, cols],
                    rhs=x_q[a][0].bitcast(FP8X4), rhs_scale=x_q[a][1][:], start=a == 0, stop=a == 1,
                )
            y1_sb = ring.tile([P, M], F32, name="y1_sb")
            nc.scalar.copy(y1_sb[:], y1_ps[:])
            factor = ring.tile([P, M], F32, name="factor", bufs=PACK)
            nc.scalar.activation(factor[:], wgo_sb[:], ACT.Copy, scale=gain_sb[:, t : t + 1])
            lesser = ring.tile([P, M], F32, name="lesser")
            nc.vector.tensor_tensor(lesser[:], y2_ps[:], y1_sb[:], ALU.min)
            page = keep.tile([P, T2], F32, name="page%d" % t)
            nc.vector.memset(page[:], 0.0)
            nc.vector.tensor_tensor(page[:].indirect(list3[:]), lesser[:], factor[:], ALU.mult)
            nc.sync.dma_start(out=out_rows[:, t, :], in_=page[:])
